import numpy as np
import ml_dtypes


def mxq(x, axis, fmt="e4m3"):
    dtype, down = {"e4m3": (ml_dtypes.float8_e4m3fn, 7), "e5m2": (ml_dtypes.float8_e5m2, 14)}[fmt]
    v = np.moveaxis(np.asarray(x, np.float32).astype(ml_dtypes.bfloat16).astype(np.float64), axis, -1)
    blocks = v.reshape(v.shape[:-1] + (-1, 32))
    amax = np.abs(blocks).max(-1, keepdims=True)
    byte = np.maximum(np.where(amax > 0, np.frexp(amax)[1] - 1 + 127, 0) - down, 1)
    scale = np.exp2(byte - 127.0)
    codes = (blocks / scale).astype(np.float32).astype(dtype).astype(np.float64)
    return np.moveaxis((codes * scale).reshape(v.shape), -1, axis)


WIDE = False


def mx_kscale(k):
    if not WIDE:
        return np.ones(k)
    levels = np.array([30, -30])
    if k % 512:
        return np.exp2(np.random.permutation(np.resize(levels, k // 32))).repeat(32)
    a = np.empty((k // 512, 16))
    for p in range(k // 512):
        a[p, :8] = np.random.permutation(np.resize(levels, 8))
        for g in range(8):
            far = levels[np.abs(levels - a[p, g]) >= 10]
            a[p, g + 8] = far[np.random.randint(len(far))]
    return np.exp2(a.ravel()).repeat(32)


def f64(x):
    return np.asarray(x).astype(np.float64)


def striped(idx):
    return np.tile(np.asarray(idx).reshape(-1, 16).T, (8, 1)).astype(np.uint16)


def unstriped(offs):
    return offs[:16].T.reshape(-1).astype(np.int64)


E2M1 = np.array([0.0, 0.5, 1.0, 1.5, 2.0, 3.0, 4.0, 6.0, -0.0, -0.5, -1.0, -1.5, -2.0, -3.0, -4.0, -6.0])


def pack_weight(w, fmt):
    k, n = w.shape
    w = f64(np.asarray(w, np.float32).astype(ml_dtypes.bfloat16)).reshape(k // 32, 32, n)
    amax = np.abs(w).max(1)
    if fmt in ("e4m3", "e5m2"):
        byte = np.frexp(amax)[1] - 1 + 127 - (7 if fmt == "e4m3" else 14)
    else:
        mant, ex = np.frexp(amax / 6.0)
        byte = np.where(mant > 0.5, ex, ex - 1) + 127
    byte = np.clip(np.where(amax > 0, byte, 1), 1, 254)
    scaled = (w * np.exp2(127.0 - byte)[:, None, :]).reshape(k, n).astype(np.float32)
    by_word = np.ascontiguousarray(scaled.reshape(k // 512, 128, 4, n).transpose(0, 1, 3, 2))
    if fmt in ("e4m3", "e5m2"):
        words = by_word.astype(ml_dtypes.float8_e4m3fn if fmt == "e4m3" else ml_dtypes.float8_e5m2).view(np.uint8)
    else:
        c = by_word.astype(ml_dtypes.float4_e2m1fn).view(np.uint8) & 0xF
        words = (c[..., 0::2] | (c[..., 1::2] << 4)).reshape(k // 512, 128, 2 * n)
    return np.ascontiguousarray(words), np.ascontiguousarray(byte.astype(np.uint8).reshape(k // 512, 16, n))


def unpack_weight(words, scales, fmt):
    g, _, n = scales.shape
    words = np.ascontiguousarray(words).reshape(g, 128, n, -1)
    if fmt in ("e4m3", "e5m2"):
        vals = words.view(ml_dtypes.float8_e4m3fn if fmt == "e4m3" else ml_dtypes.float8_e5m2).astype(np.float64)
    else:
        nib = np.empty((g, 128, n, 4), np.uint8)
        nib[..., 0::2] = words & 0xF
        nib[..., 1::2] = words >> 4
        vals = E2M1[nib]
    vals = vals * np.repeat(np.exp2(scales.astype(np.float64) - 127.0), 8, axis=1)[..., None]
    return vals.transpose(0, 1, 3, 2).reshape(g * 512, n)


K, T, J, I, G = 1024, 1024, 256, 256, 32


def setup_inputs():
    n = np.random.standard_normal
    idx = np.random.permutation(T)[:J]
    fk = mx_kscale(K)
    kyp = pack_weight(n((K, I)) / fk[:, None], "e5m2")
    return {
        "xf": (n((K, T)) * 0.03).astype(np.float32),
        "fk": (np.random.uniform(0.5, 2.0, (K, 1)) * fk[:, None]).astype(np.float32),
        "ky_words": kyp[0],
        "ky_scales": kyp[1],
        "bi": (np.random.uniform(-0.7, 0.7, (1, I))).astype(np.float32),
        "offs": striped(idx),
    }


def reference(xf, fk, ky_words, ky_scales, bi, offs):
    idx = unstriped(offs)
    kyu = unpack_weight(ky_words, ky_scales, "e5m2")
    xg = f64(xf)[:, idx]
    x1 = np.pad(xg, ((0, 0), (1, 0)))[:, :J]
    u = (xg - 0.6 * x1) * f64(fk)
    uq = mxq(u, 0, "e5m2")
    a0 = uq.T @ kyu
    a = a0 + f64(bi)
    g1 = a.reshape(J, G, I // G).max(axis=2)
    y = g1 - 0.5 * np.max(a, axis=1, keepdims=True)
    return y

@@ -1,0 +1,174 @@
+from contextlib import ExitStack
+
+import concourse.mybir as mybir
+from concourse.masks import make_identity
+
+K, T, J, I, G = 1024, 1024, 256, 256, 32
+FLOPS = 2 * K * J * I
+
+F32 = mybir.dt.float32
+BF16 = mybir.dt.bfloat16
+U32 = mybir.dt.uint32
+I32 = mybir.dt.int32
+U16 = mybir.dt.uint16
+U8 = mybir.dt.uint8
+E5M2X4 = mybir.dt.float8_e5m2_x4
+ALU = mybir.AluOpType
+ACT = mybir.ActivationFunctionType
+AX = mybir.AxisListType
+
+P = 128
+PACK = 4
+PASSES = K // (P * PACK)
+HALVES = J // P
+PAD = 8
+LIST_ROWS = 16
+
+
+def tile_list_scores_steps_given_bundles_kernel(tc, xf, fk, ky_words, ky_scales, bi, offs, out):
+    nc = tc.nc
+    with ExitStack() as ctx:
+        keep = ctx.enter_context(tc.tile_pool(name="keep", bufs=1))
+        psum = ctx.enter_context(tc.psum_pool(name="psum", bufs=1))
+
+        offsets = keep.tile([P, J // LIST_ROWS], U16, name="offsets")
+        nc.sync.dma_start(offsets[:], offs)
+
+        factor = keep.tile([P, PASSES, PACK], F32, name="factor")
+        nc.scalar.dma_start(factor[:], fk.rearrange("(a p t) o -> p a (t o)", p=P, t=PACK))
+        bias_col = keep.tile([P, 2], F32, name="bias_col")
+        nc.scalar.dma_start(bias_col[:], bi.rearrange("o (p c) -> p (o c)", c=2))
+
+        rows = xf.rearrange("(a p t) n -> a t p n", p=P, t=PACK)
+        planes = []
+        for a in range(PASSES):
+            for t in range(PACK):
+                plane = keep.tile([P, T], F32, name="plane%d%d" % (a, t))
+                nc.sync.dma_start(plane[:], rows[a, t])
+                planes.append(plane)
+
+        key_words = keep.tile([P, PASSES, I], U32, name="key_words", align_bytes=64)
+        nc.sync.dma_start(
+            key_words[:].bitcast(I32),
+            ky_words.rearrange("z p c r -> p z (c r)").bitcast(I32),
+        )
+
+        ident = keep.tile([P, P], F32, name="ident")
+        make_identity(nc, ident[:])
+        key_scales = keep.tile([P, PASSES, I], U8, name="key_scales", align_bytes=64)
+        nc.vector.memset(key_scales[:].bitcast(I32), 0)
+        for q in range(4):
+            nc.gpsimd.dma_start(
+                key_scales[32 * q : 32 * q + 4].bitcast(I32),
+                ky_scales[:, 4 * q : 4 * q + 4, :].rearrange("z r c -> r z c").bitcast(I32),
+            )
+
+        zero = keep.tile([P, 1], F32, name="zero")
+        nc.vector.memset(zero[:], 0.0)
+        picked = []
+        for n in range(PASSES * PACK):
+            g = keep.tile([P, PAD + J], F32, name="picked%d" % n)
+            nc.scalar.activation(out=g[:, PAD - 1 : PAD], in_=zero[:], func=ACT.Copy)
+            picked.append(g)
+
+        bias_ps = psum.tile([P, 2, P], F32, name="bias_ps")
+        for c in range(2):
+            nc.tensor.transpose(bias_ps[:, c, :], bias_col[:, c : c + 1].to_broadcast([P, P]), ident[:])
+        bias = keep.tile([P, I], F32, name="bias")
+        nc.vector.tensor_copy(
+            out=bias[:].rearrange("p (n c) -> p n c", c=2),
+            in_=bias_ps[:].rearrange("p c n -> p n c"),
+        )
+
+        acc = [psum.tile([P, I], F32, name="acc%d" % h) for h in range(HALVES)]
+
+        def gather(engine, n, j0, j1):
+            src = planes[n][:].indirect(offsets[:, j0 // LIST_ROWS : j1 // LIST_ROWS])
+            dst = picked[n][:, PAD + j0 : PAD + j1]
+            if engine == "vector":
+                nc.vector.tensor_copy(dst, src)
+            else:
+                nc.scalar.activation(out=dst, in_=src, func=ACT.Copy)
+
+        def step(n, diff, j0, j1):
+            nc.vector.scalar_tensor_tensor(
+                out=diff[:, j0:j1],
+                in0=picked[n][:, PAD - 1 + j0 : PAD - 1 + j1],
+                scalar=-0.6,
+                in1=picked[n][:, PAD + j0 : PAD + j1],
+                op0=ALU.mult,
+                op1=ALU.add,
+            )
+
+        def scale(n, diff, grouped, j0, j1):
+            a, t = divmod(n, PACK)
+            nc.vector.tensor_scalar(
+                out=grouped[:, :, t],
+                in0=diff[:, j0:j1],
+                scalar1=factor[:, a, t : t + 1],
+                scalar2=None,
+                op0=ALU.mult,
+            )
+
+        def quantise(grouped, width, name):
+            codes = keep.tile([P, width], U32, name="codes" + name, align_bytes=64)
+            scales = keep.tile([P, width], U8, name="scales" + name, align_bytes=64)
+            nc.vector.quantize_mx(
+                out=codes[:].bitcast(E5M2X4),
+                scales=scales[:],
+                in_=grouped[:].rearrange("p j t -> p (j t)"),
+            )
+            return codes, scales
+
+        def multiply(a, h, codes, scales):
+            nc.tensor.matmul_mx(
+                out=acc[h][:],
+                lhsT=codes.bitcast(E5M2X4),
+                lhsT_scale=scales,
+                rhs=key_words[:, a, :].bitcast(E5M2X4),
+                rhs_scale=key_scales[:, a, :],
+                start=(a == 0),
+                stop=(a == PASSES - 1),
+            )
+
+        diffs = [keep.tile([P, J], F32, name="diff%d" % n) for n in range(PASSES * PACK)]
+        for a in range(PASSES):
+            grouped = [
+                keep.tile([P, P, PACK], BF16, name="grouped%d%d" % (a, h), align_bytes=64)
+                for h in range(HALVES)
+            ]
+            for t in range(PACK):
+                n = a * PACK + t
+                for h in range(HALVES):
+                    gather("scalar", n, h * P, (h + 1) * P)
+                for h in range(HALVES):
+                    step(n, diffs[n], h * P, (h + 1) * P)
+                for h in range(HALVES):
+                    scale(n, diffs[n], grouped[h], h * P, (h + 1) * P)
+            for h in range(HALVES):
+                codes, scales = quantise(grouped[h], P, "%d%d" % (a, h))
+                multiply(a, h, codes[:], scales[:])
+
+        scores = [keep.tile([P, I], F32, name="scores%d" % h) for h in range(HALVES)]
+        bundle_max = keep.tile([P, HALVES, G], F32, name="bundle_max")
+        row_max = keep.tile([P, HALVES], F32, name="row_max")
+        result = keep.tile([P, HALVES, G], F32, name="result")
+        for h in range(HALVES):
+            nc.vector.tensor_tensor(out=scores[h][:], in0=acc[h][:], in1=bias[:], op=ALU.add)
+        for h in range(HALVES):
+            nc.vector.tensor_reduce(
+                out=bundle_max[:, h, :],
+                in_=scores[h][:].rearrange("p (g r) -> p g r", g=G),
+                axis=AX.X,
+                op=ALU.max,
+            )
+        nc.vector.tensor_reduce(out=row_max[:], in_=bundle_max[:], axis=AX.X, op=ALU.max)
+        nc.vector.scalar_tensor_tensor(
+            out=result[:],
+            in0=row_max[:].unsqueeze(2).to_broadcast([P, HALVES, G]),
+            scalar=-0.5,
+            in1=bundle_max[:],
+            op0=ALU.mult,
+            op1=ALU.add,
+        )
+        nc.sync.dma_start(out.rearrange("(h p) g -> p h g", p=P), result[:])

@@ -58,7 +58,7 @@ def tile_list_scores_steps_given_bundles_kernel(tc, xf, fk, ky_words, ky_scales,
         key_scales = keep.tile([P, PASSES, I], U8, name="key_scales", align_bytes=64)
         nc.vector.memset(key_scales[:].bitcast(I32), 0)
         for q in range(4):
-            nc.gpsimd.dma_start(
+            nc.sync.dma_start(
                 key_scales[32 * q : 32 * q + 4].bitcast(I32),
                 ky_scales[:, 4 * q : 4 * q + 4, :].rearrange("z r c -> r z c").bitcast(I32),
             )

@@ -32,20 +32,30 @@ def tile_list_scores_steps_given_bundles_kernel(tc, xf, fk, ky_words, ky_scales,
         psum = ctx.enter_context(tc.psum_pool(name="psum", bufs=1))
 
         offsets = keep.tile([P, J // LIST_ROWS], U16, name="offsets")
+        rows = xf.rearrange("(a p t) n -> a p t n", p=P, t=PACK)
+        first = keep.tile([P, T], F32, name="plane0")
+        nc.sync.dma_start(first[:], rows[0, :, 0, :])
         nc.sync.dma_start(offsets[:], offs)
+        planes = [first[:]]
 
-        factor = keep.tile([P, PASSES, PACK], F32, name="factor")
-        nc.scalar.dma_start(factor[:], fk.rearrange("(a p t) o -> p a (t o)", p=P, t=PACK))
+        factor = keep.tile([P, PASSES, 2 * PACK], F32, name="factor")
+        nc.scalar.dma_start(factor[:, :, 0:PACK], fk.rearrange("(a p t) o -> p a (t o)", p=P, t=PACK))
+
+        for n in range(1, PASSES * PACK):
+            plane = keep.tile([P, T], F32, name="plane%d" % n)
+            nc.sync.dma_start(plane[:], rows[n // PACK, :, n % PACK, :])
+            planes.append(plane[:])
+
+        key_scales = keep.tile([P, PASSES, I], U8, name="key_scales", align_bytes=64)
+        nc.vector.memset(key_scales[:].bitcast(I32), 0)
+        for q in range(4):
+            nc.sync.dma_start(
+                key_scales[32 * q : 32 * q + 4].bitcast(I32),
+                ky_scales[:, 4 * q : 4 * q + 4, :].rearrange("z r c -> r z c").bitcast(I32),
+            )
+
         bias_col = keep.tile([P, 2], F32, name="bias_col")
-        nc.scalar.dma_start(bias_col[:], bi.rearrange("o (p c) -> p (o c)", c=2))
-
-        rows = xf.rearrange("(a p t) n -> a t p n", p=P, t=PACK)
-        planes = []
-        for a in range(PASSES):
-            for t in range(PACK):
-                plane = keep.tile([P, T], F32, name="plane%d%d" % (a, t))
-                nc.sync.dma_start(plane[:], rows[a, t])
-                planes.append(plane)
+        nc.sync.dma_start(bias_col[:], bi.rearrange("o (p c) -> p (o c)", c=2))
 
         key_words = keep.tile([P, PASSES, I], U32, name="key_words", align_bytes=64)
         nc.sync.dma_start(
@@ -55,14 +65,6 @@ def tile_list_scores_steps_given_bundles_kernel(tc, xf, fk, ky_words, ky_scales,
 
         ident = keep.tile([P, P], F32, name="ident")
         make_identity(nc, ident[:])
-        key_scales = keep.tile([P, PASSES, I], U8, name="key_scales", align_bytes=64)
-        nc.vector.memset(key_scales[:].bitcast(I32), 0)
-        for q in range(4):
-            nc.sync.dma_start(
-                key_scales[32 * q : 32 * q + 4].bitcast(I32),
-                ky_scales[:, 4 * q : 4 * q + 4, :].rearrange("z r c -> r z c").bitcast(I32),
-            )
-
         zero = keep.tile([P, 1], F32, name="zero")
         nc.vector.memset(zero[:], 0.0)
         picked = []
@@ -71,19 +73,10 @@ def tile_list_scores_steps_given_bundles_kernel(tc, xf, fk, ky_words, ky_scales,
             nc.scalar.activation(out=g[:, PAD - 1 : PAD], in_=zero[:], func=ACT.Copy)
             picked.append(g)
 
-        bias_ps = psum.tile([P, 2, P], F32, name="bias_ps")
-        for c in range(2):
-            nc.tensor.transpose(bias_ps[:, c, :], bias_col[:, c : c + 1].to_broadcast([P, P]), ident[:])
-        bias = keep.tile([P, I], F32, name="bias")
-        nc.vector.tensor_copy(
-            out=bias[:].rearrange("p (n c) -> p n c", c=2),
-            in_=bias_ps[:].rearrange("p c n -> p n c"),
-        )
-
         acc = [psum.tile([P, I], F32, name="acc%d" % h) for h in range(HALVES)]
 
         def gather(engine, n, j0, j1):
-            src = planes[n][:].indirect(offsets[:, j0 // LIST_ROWS : j1 // LIST_ROWS])
+            src = planes[n].indirect(offsets[:, j0 // LIST_ROWS : j1 // LIST_ROWS])
             dst = picked[n][:, PAD + j0 : PAD + j1]
             if engine == "vector":
                 nc.vector.tensor_copy(dst, src)
@@ -149,26 +142,38 @@ def tile_list_scores_steps_given_bundles_kernel(tc, xf, fk, ky_words, ky_scales,
                 codes, scales = quantise(grouped[h], P, "%d%d" % (a, h))
                 multiply(a, h, codes[:], scales[:])
 
+        bias_ps = psum.tile([P, 2, P], F32, name="bias_ps")
+        for c in range(2):
+            nc.tensor.transpose(bias_ps[:, c, :], bias_col[:, c : c + 1].to_broadcast([P, P]), ident[:])
+        bias = keep.tile([P, I], F32, name="bias")
+        nc.scalar.copy(
+            out=bias[:].rearrange("p (n c) -> p n c", c=2),
+            in_=bias_ps[:].rearrange("p c n -> p n c"),
+        )
+
         scores = [keep.tile([P, I], F32, name="scores%d" % h) for h in range(HALVES)]
-        bundle_max = keep.tile([P, HALVES, G], F32, name="bundle_max")
-        row_max = keep.tile([P, HALVES], F32, name="row_max")
-        result = keep.tile([P, HALVES, G], F32, name="result")
+        bundle_max = [keep.tile([P, G], F32, name="bundle_max%d" % h) for h in range(HALVES)]
+        row_max = [keep.tile([P, 1], F32, name="row_max%d" % h) for h in range(HALVES)]
+        result = [keep.tile([P, G], F32, name="result%d" % h) for h in range(HALVES)]
         for h in range(HALVES):
             nc.vector.tensor_tensor(out=scores[h][:], in0=acc[h][:], in1=bias[:], op=ALU.add)
         for h in range(HALVES):
             nc.vector.tensor_reduce(
-                out=bundle_max[:, h, :],
+                out=bundle_max[h][:],
                 in_=scores[h][:].rearrange("p (g r) -> p g r", g=G),
                 axis=AX.X,
                 op=ALU.max,
             )
-        nc.vector.tensor_reduce(out=row_max[:], in_=bundle_max[:], axis=AX.X, op=ALU.max)
-        nc.vector.scalar_tensor_tensor(
-            out=result[:],
-            in0=row_max[:].unsqueeze(2).to_broadcast([P, HALVES, G]),
-            scalar=-0.5,
-            in1=bundle_max[:],
-            op0=ALU.mult,
-            op1=ALU.add,
-        )
-        nc.sync.dma_start(out.rearrange("(h p) g -> p h g", p=P), result[:])
+        for h in range(HALVES):
+            nc.vector.tensor_reduce(out=row_max[h][:], in_=bundle_max[h][:], axis=AX.X, op=ALU.max)
+        for h in range(HALVES):
+            nc.vector.scalar_tensor_tensor(
+                out=result[h][:],
+                in0=row_max[h][:].to_broadcast([P, G]),
+                scalar=-0.5,
+                in1=bundle_max[h][:],
+                op0=ALU.mult,
+                op1=ALU.add,
+            )
+            queue = nc.scalar if h == 0 else nc.sync
+            queue.dma_start(out[h * P : (h + 1) * P, :], result[h][:])

from contextlib import ExitStack

import concourse.mybir as mybir
from concourse.masks import make_identity

K, T, J, I, G = 1024, 1024, 256, 256, 32
FLOPS = 2 * K * J * I

F32 = mybir.dt.float32
BF16 = mybir.dt.bfloat16
U32 = mybir.dt.uint32
I32 = mybir.dt.int32
U16 = mybir.dt.uint16
U8 = mybir.dt.uint8
E5M2X4 = mybir.dt.float8_e5m2_x4
ALU = mybir.AluOpType
ACT = mybir.ActivationFunctionType
AX = mybir.AxisListType

P = 128
PACK = 4
PASSES = K // (P * PACK)
HALVES = J // P
PAD = 8
LIST_ROWS = 16


def tile_list_scores_steps_given_bundles_kernel(tc, xf, fk, ky_words, ky_scales, bi, offs, out):
    nc = tc.nc
    with ExitStack() as ctx:
        keep = ctx.enter_context(tc.tile_pool(name="keep", bufs=1))
        psum = ctx.enter_context(tc.psum_pool(name="psum", bufs=1))

        offsets = keep.tile([P, J // LIST_ROWS], U16, name="offsets")
        rows = xf.rearrange("(a p t) n -> a p t n", p=P, t=PACK)
        first = keep.tile([P, T], F32, name="plane0")
        nc.sync.dma_start(first[:], rows[0, :, 0, :])
        nc.sync.dma_start(offsets[:], offs)
        planes = [first[:]]

        factor = keep.tile([P, PASSES, 2 * PACK], F32, name="factor")
        nc.scalar.dma_start(factor[:, :, 0:PACK], fk.rearrange("(a p t) o -> p a (t o)", p=P, t=PACK))

        for n in range(1, PASSES * PACK):
            plane = keep.tile([P, T], F32, name="plane%d" % n)
            nc.sync.dma_start(plane[:], rows[n // PACK, :, n % PACK, :])
            planes.append(plane[:])

        key_scales = keep.tile([P, PASSES, I], U8, name="key_scales", align_bytes=64)
        nc.vector.memset(key_scales[:].bitcast(I32), 0)
        for q in range(4):
            nc.sync.dma_start(
                key_scales[32 * q : 32 * q + 4].bitcast(I32),
                ky_scales[:, 4 * q : 4 * q + 4, :].rearrange("z r c -> r z c").bitcast(I32),
            )

        bias_col = keep.tile([P, 2], F32, name="bias_col")
        nc.sync.dma_start(bias_col[:], bi.rearrange("o (p c) -> p (o c)", c=2))

        key_words = keep.tile([P, PASSES, I], U32, name="key_words", align_bytes=64)
        nc.sync.dma_start(
            key_words[:].bitcast(I32),
            ky_words.rearrange("z p c r -> p z (c r)").bitcast(I32),
        )

        ident = keep.tile([P, P], F32, name="ident")
        make_identity(nc, ident[:])
        zero = keep.tile([P, 1], F32, name="zero")
        nc.vector.memset(zero[:], 0.0)
        picked = []
        for n in range(PASSES * PACK):
            g = keep.tile([P, PAD + J], F32, name="picked%d" % n)
            nc.scalar.activation(out=g[:, PAD - 1 : PAD], in_=zero[:], func=ACT.Copy)
            picked.append(g)

        acc = [psum.tile([P, I], F32, name="acc%d" % h) for h in range(HALVES)]

        def gather(engine, n, j0, j1):
            src = planes[n].indirect(offsets[:, j0 // LIST_ROWS : j1 // LIST_ROWS])
            dst = picked[n][:, PAD + j0 : PAD + j1]
            if engine == "vector":
                nc.vector.tensor_copy(dst, src)
            else:
                nc.scalar.activation(out=dst, in_=src, func=ACT.Copy)

        def step(n, diff, j0, j1):
            nc.vector.scalar_tensor_tensor(
                out=diff[:, j0:j1],
                in0=picked[n][:, PAD - 1 + j0 : PAD - 1 + j1],
                scalar=-0.6,
                in1=picked[n][:, PAD + j0 : PAD + j1],
                op0=ALU.mult,
                op1=ALU.add,
            )

        def scale(n, diff, grouped, j0, j1):
            a, t = divmod(n, PACK)
            nc.vector.tensor_scalar(
                out=grouped[:, :, t],
                in0=diff[:, j0:j1],
                scalar1=factor[:, a, t : t + 1],
                scalar2=None,
                op0=ALU.mult,
            )

        def quantise(grouped, width, name):
            codes = keep.tile([P, width], U32, name="codes" + name, align_bytes=64)
            scales = keep.tile([P, width], U8, name="scales" + name, align_bytes=64)
            nc.vector.quantize_mx(
                out=codes[:].bitcast(E5M2X4),
                scales=scales[:],
                in_=grouped[:].rearrange("p j t -> p (j t)"),
            )
            return codes, scales

        def multiply(a, h, codes, scales):
            nc.tensor.matmul_mx(
                out=acc[h][:],
                lhsT=codes.bitcast(E5M2X4),
                lhsT_scale=scales,
                rhs=key_words[:, a, :].bitcast(E5M2X4),
                rhs_scale=key_scales[:, a, :],
                start=(a == 0),
                stop=(a == PASSES - 1),
            )

        diffs = [keep.tile([P, J], F32, name="diff%d" % n) for n in range(PASSES * PACK)]
        for a in range(PASSES):
            grouped = [
                keep.tile([P, P, PACK], BF16, name="grouped%d%d" % (a, h), align_bytes=64)
                for h in range(HALVES)
            ]
            for t in range(PACK):
                n = a * PACK + t
                for h in range(HALVES):
                    gather("scalar", n, h * P, (h + 1) * P)
                for h in range(HALVES):
                    step(n, diffs[n], h * P, (h + 1) * P)
                for h in range(HALVES):
                    scale(n, diffs[n], grouped[h], h * P, (h + 1) * P)
            for h in range(HALVES):
                codes, scales = quantise(grouped[h], P, "%d%d" % (a, h))
                multiply(a, h, codes[:], scales[:])

        bias_ps = psum.tile([P, 2, P], F32, name="bias_ps")
        for c in range(2):
            nc.tensor.transpose(bias_ps[:, c, :], bias_col[:, c : c + 1].to_broadcast([P, P]), ident[:])
        bias = keep.tile([P, I], F32, name="bias")
        nc.scalar.copy(
            out=bias[:].rearrange("p (n c) -> p n c", c=2),
            in_=bias_ps[:].rearrange("p c n -> p n c"),
        )

        scores = [keep.tile([P, I], F32, name="scores%d" % h) for h in range(HALVES)]
        bundle_max = [keep.tile([P, G], F32, name="bundle_max%d" % h) for h in range(HALVES)]
        row_max = [keep.tile([P, 1], F32, name="row_max%d" % h) for h in range(HALVES)]
        result = [keep.tile([P, G], F32, name="result%d" % h) for h in range(HALVES)]
        for h in range(HALVES):
            nc.vector.tensor_tensor(out=scores[h][:], in0=acc[h][:], in1=bias[:], op=ALU.add)
        for h in range(HALVES):
            nc.vector.tensor_reduce(
                out=bundle_max[h][:],
                in_=scores[h][:].rearrange("p (g r) -> p g r", g=G),
                axis=AX.X,
                op=ALU.max,
            )
        for h in range(HALVES):
            nc.vector.tensor_reduce(out=row_max[h][:], in_=bundle_max[h][:], axis=AX.X, op=ALU.max)
        for h in range(HALVES):
            nc.vector.scalar_tensor_tensor(
                out=result[h][:],
                in0=row_max[h][:].to_broadcast([P, G]),
                scalar=-0.5,
                in1=bundle_max[h][:],
                op0=ALU.mult,
                op1=ALU.add,
            )
            queue = nc.scalar if h == 0 else nc.sync
            queue.dma_start(out[h * P : (h + 1) * P, :], result[h][:])
